import numpy as np
import ml_dtypes


def mxq(x, axis, fmt="e4m3"):
    dtype, down = {"e4m3": (ml_dtypes.float8_e4m3fn, 7), "e5m2": (ml_dtypes.float8_e5m2, 14)}[fmt]
    v = np.moveaxis(np.asarray(x, np.float32).astype(ml_dtypes.bfloat16).astype(np.float64), axis, -1)
    blocks = v.reshape(v.shape[:-1] + (-1, 32))
    amax = np.abs(blocks).max(-1, keepdims=True)
    byte = np.maximum(np.where(amax > 0, np.frexp(amax)[1] - 1 + 127, 0) - down, 1)
    scale = np.exp2(byte - 127.0)
    codes = (blocks / scale).astype(np.float32).astype(dtype).astype(np.float64)
    return np.moveaxis((codes * scale).reshape(v.shape), -1, axis)


WIDE = False


def mx_kscale(k):
    if not WIDE:
        return np.ones(k)
    levels = np.array([10, -10, 5, -5, 0])
    if k % 512:
        return np.exp2(np.random.permutation(np.resize(levels, k // 32))).repeat(32)
    a = np.empty((k // 512, 16))
    for p in range(k // 512):
        a[p, :8] = np.random.permutation(np.resize(levels, 8))
        for g in range(8):
            far = levels[np.abs(levels - a[p, g]) >= 10]
            a[p, g + 8] = far[np.random.randint(len(far))]
    return np.exp2(a.ravel()).repeat(32)


def f64(x):
    return np.asarray(x).astype(np.float64)


def striped(idx):
    return np.tile(np.asarray(idx).reshape(-1, 16).T, (8, 1)).astype(np.uint16)


def unstriped(offs):
    return offs[:16].T.reshape(-1).astype(np.int64)


E2M1 = np.array([0.0, 0.5, 1.0, 1.5, 2.0, 3.0, 4.0, 6.0, -0.0, -0.5, -1.0, -1.5, -2.0, -3.0, -4.0, -6.0])


def pack_weight(w, fmt):
    k, n = w.shape
    w = f64(np.asarray(w, np.float32).astype(ml_dtypes.bfloat16)).reshape(k // 32, 32, n)
    amax = np.abs(w).max(1)
    if fmt == "e4m3":
        byte = np.frexp(amax)[1] - 1 + 127 - 7
    else:
        mant, ex = np.frexp(amax / 6.0)
        byte = np.where(mant > 0.5, ex, ex - 1) + 127
    byte = np.clip(np.where(amax > 0, byte, 1), 1, 254)
    scaled = (w * np.exp2(127.0 - byte)[:, None, :]).reshape(k, n).astype(np.float32)
    by_word = np.ascontiguousarray(scaled.reshape(k // 512, 128, 4, n).transpose(0, 1, 3, 2))
    if fmt == "e4m3":
        words = by_word.astype(ml_dtypes.float8_e4m3fn).view(np.uint8)
    else:
        c = by_word.astype(ml_dtypes.float4_e2m1fn).view(np.uint8) & 0xF
        words = (c[..., 0::2] | (c[..., 1::2] << 4)).reshape(k // 512, 128, 2 * n)
    return np.ascontiguousarray(words), np.ascontiguousarray(byte.astype(np.uint8).reshape(k // 512, 16, n))


def unpack_weight(words, scales, fmt):
    g, _, n = scales.shape
    words = np.ascontiguousarray(words).reshape(g, 128, n, -1)
    if fmt == "e4m3":
        vals = words.view(ml_dtypes.float8_e4m3fn).astype(np.float64)
    else:
        nib = np.empty((g, 128, n, 4), np.uint8)
        nib[..., 0::2] = words & 0xF
        nib[..., 1::2] = words >> 4
        vals = E2M1[nib]
    vals = vals * np.repeat(np.exp2(scales.astype(np.float64) - 127.0), 8, axis=1)[..., None]
    return vals.transpose(0, 1, 3, 2).reshape(g * 512, n)


D, T, I, Q, E, U, G = 512, 2048, 512, 256, 512, 1024, 64


def setup_inputs():
    n = np.random.standard_normal
    idx = np.random.permutation(T)[:I]
    idx2 = np.random.permutation(U)[:I]
    fd = mx_kscale(D)
    fi = mx_kscale(I)
    ti = np.ones(T)
    ti[idx] = fi
    keysp = pack_weight(n((D, T)) / fd[:, None], "e4m3")
    return {
        "query": (n((D, Q)) * 0.9 / np.sqrt(D) * fd[:, None]).astype(np.float32),
        "keys_words": keysp[0],
        "keys_scales": keysp[1],
        "query2": (n((D, Q)) * 0.9 / np.sqrt(D) * fd[:, None]).astype(np.float32),
        "notes": (n((D, U)) / fd[:, None]).astype(np.float32),
        "lam": (np.random.uniform(0.1, 0.5, (Q, 1))).astype(np.float32),
        "shy": (np.random.uniform(20.0, 60.0, (Q, 1))).astype(np.float32),
        "os": (np.random.uniform(4.0, 16.0, (1, I)) * fi).astype(np.float32),
        "vals": (n((E, T)) / ti).astype(np.float32),
        "memq": (np.random.uniform(0.3, 1.0, (1, Q))).astype(np.float32),
        "offs": striped(idx),
        "offs2": striped(idx2),
    }


def reference(query, keys_words, keys_scales, query2, notes, lam, shy, os, vals, memq, offs, offs2):
    idx = unstriped(offs)
    idx2 = unstriped(offs2)
    keysu = unpack_weight(keys_words, keys_scales, "e4m3")
    queryq = mxq(f64(query), 0, "e4m3")
    keysidxg = keysu[:, idx]
    a = queryq.T @ keysidxg
    query2q = mxq(f64(query2), 0, "e4m3")
    notesidx2q = mxq(f64(notes)[:, idx2], 0, "e4m3")
    b = query2q.T @ notesidx2q
    s = np.maximum(a, b) + np.minimum(a, b) * f64(lam)
    p = np.exp(s - np.max(s, axis=1, keepdims=True))
    r = p / np.sum(p, axis=1, keepdims=True)
    pg = r.reshape(Q, G, I // G).sum(axis=2)
    k0 = np.exp(pg * f64(shy) * (-1.0))
    kr = np.repeat(k0, I // G, axis=1)
    u0 = r * kr
    w = u0 / np.sum(u0, axis=1, keepdims=True)
    wo1 = w * f64(os)
    wt1 = wo1.T
    vt1 = f64(vals)[:, idx].T
    vt1q = mxq(vt1, 0, "e4m3")
    wt1q = mxq(wt1, 0, "e4m3")
    o = vt1q.T @ wt1q
    o1 = np.pad(o, ((0, 0), (1, 0)))[:, :Q]
    y = o - o1 * f64(memq)
    return y

@@ -1,0 +1,240 @@
+from contextlib import ExitStack
+
+import concourse.mybir as mybir
+from concourse.masks import make_identity
+
+D, T, I, Q, E, U, G = 512, 2048, 512, 256, 512, 1024, 64
+FLOPS = 2 * (2 * D * Q * I + I * E * Q)
+
+F32 = mybir.dt.float32
+BF16 = mybir.dt.bfloat16
+I32 = mybir.dt.int32
+U32 = mybir.dt.uint32
+U16 = mybir.dt.uint16
+U8 = mybir.dt.uint8
+FP8X4 = mybir.dt.float8_e4m3fn_x4
+ALU = mybir.AluOpType
+ACT = mybir.ActivationFunctionType
+AX = mybir.AxisListType
+
+P = 128
+PACK = 4
+RUN = I // G
+Q_TILES = Q // P
+E_TILES = E // P
+
+
+def interleave(engine_copy, grouped, planes):
+    engine_copy(
+        out=grouped.rearrange("p (c i) t -> p c t i", i=4),
+        in_=planes.rearrange("p t (c i) -> p c t i", i=4),
+    )
+
+
+def quantize(nc, codes, scales, grouped):
+    nc.vector.quantize_mx(out=codes.bitcast(FP8X4), scales=scales, in_=grouped.rearrange("p c t -> p (c t)"))
+
+
+def tile_attend_twopools_crowdshy_rowchanges_kernel(
+    tc, query, keys_words, keys_scales, query2, notes, lam, shy, slot_factor, vals, memq, offs, offs2, out
+):
+    nc = tc.nc
+    with ExitStack() as ctx:
+        lists = ctx.enter_context(tc.tile_pool(name="lists", bufs=1))
+        keep = ctx.enter_context(tc.tile_pool(name="keep", bufs=1))
+        work = ctx.enter_context(tc.tile_pool(name="work", bufs=2))
+        psum = ctx.enter_context(tc.psum_pool(name="psum", bufs=2))
+
+        offs_t = lists.tile([P, I // 16], U16, name="offs_t")
+        offs2_t = lists.tile([P, I // 16], U16, name="offs2_t")
+
+        key_scale_pool = keep.tile([P, T], U8, name="key_scale_pool", align_bytes=64)
+        nc.vector.memset(key_scale_pool[:].bitcast(I32), 0)
+
+        notes_rows = notes.rearrange("(p t) u -> p t u", t=PACK)
+        note_pool = [keep.tile([P, U], F32, name=f"note_pool{t}") for t in range(PACK)]
+        nc.sync.dma_start(out=note_pool[0][:], in_=notes_rows[:, 0, :])
+        nc.sync.dma_start(offs2_t[:], offs2)
+        for t in range(1, PACK):
+            nc.sync.dma_start(out=note_pool[t][:], in_=notes_rows[:, t, :])
+        nc.sync.dma_start(offs_t[:], offs)
+        for quad in range(4):
+            nc.sync.dma_start(
+                out=key_scale_pool[32 * quad : 32 * quad + 4, :].bitcast(I32),
+                in_=keys_scales[0, 4 * quad : 4 * quad + 4, :].bitcast(I32),
+            )
+        q2_raw = keep.tile([P, PACK, Q], F32, name="q2_raw")
+        nc.sync.dma_start(out=q2_raw[:], in_=query2.rearrange("(p t) q -> p t q", t=PACK))
+        q1_raw = keep.tile([P, PACK, Q], F32, name="q1_raw")
+        nc.sync.dma_start(out=q1_raw[:], in_=query.rearrange("(p t) q -> p t q", t=PACK))
+        key_word_pool = keep.tile([P, T], U32, name="key_word_pool", align_bytes=64)
+        nc.sync.dma_start(
+            out=key_word_pool[:].bitcast(I32), in_=keys_words[0].rearrange("p n t -> p (n t)").bitcast(I32)
+        )
+        lam_col = keep.tile([P, Q_TILES], F32, name="lam_col")
+        shy_col = keep.tile([P, Q_TILES], F32, name="shy_col")
+        with nc.allow_non_contiguous_dma(reason="one value a query row, rows on the partitions"):
+            nc.sync.dma_start(out=lam_col[:], in_=lam.rearrange("(h p) o -> p (h o)", p=P))
+            nc.sync.dma_start(out=shy_col[:], in_=shy.rearrange("(h p) o -> p (h o)", p=P))
+        factor_col = keep.tile([P, PACK], F32, name="factor_col")
+        nc.sync.dma_start(out=factor_col[:], in_=slot_factor.rearrange("o (p t) -> p (o t)", t=PACK))
+        mem_col = keep.tile([P, 2], F32, name="mem_col")
+        nc.sync.dma_start(out=mem_col[:], in_=memq.rearrange("o (p t) -> p (o t)", t=2))
+        val_pool = [keep.tile([P, T], F32, name=f"val_pool{j}") for j in range(E_TILES)]
+        for j in range(E_TILES):
+            nc.sync.dma_start(out=val_pool[j][:], in_=vals[j * P : (j + 1) * P, :])
+
+        ident = keep.tile([P, P], F32, name="ident")
+        make_identity(nc, ident[:])
+
+        note_planes = keep.tile([P, PACK, I], BF16, name="note_planes", align_bytes=64)
+        half = I // 2
+        nc.vector.tensor_copy(note_planes[:, 0, :], note_pool[0][:].indirect(offs2_t[:]))
+        nc.scalar.activation(note_planes[:, 1, :], note_pool[1][:].indirect(offs2_t[:]), ACT.Copy)
+        nc.vector.tensor_copy(note_planes[:, 2, :], note_pool[2][:].indirect(offs2_t[:]))
+        nc.vector.tensor_copy(note_planes[:, 3, :half], note_pool[3][:].indirect(offs2_t[:, : half // 16]))
+        nc.scalar.activation(note_planes[:, 3, half:], note_pool[3][:].indirect(offs2_t[:, half // 16 :]), ACT.Copy)
+        note_grouped = keep.tile([P, I, PACK], BF16, name="note_grouped", align_bytes=64)
+        interleave(nc.vector.tensor_copy, note_grouped[:], note_planes[:])
+        note_codes = keep.tile([P, I], U32, name="note_codes", align_bytes=64)
+        note_scales = keep.tile([P, I], U8, name="note_scales", align_bytes=64)
+        quantize(nc, note_codes[:], note_scales[:], note_grouped[:])
+
+        q_codes, q_scales = [], []
+        for n, raw in enumerate((q2_raw, q1_raw)):
+            grouped = keep.tile([P, Q, PACK], BF16, name=f"q_grouped{n}", align_bytes=64)
+            interleave(nc.scalar.copy, grouped[:], raw[:])
+            codes = keep.tile([P, Q], U32, name=f"q_codes{n}", align_bytes=64)
+            scales = keep.tile([P, Q], U8, name=f"q_scales{n}", align_bytes=64)
+            q_codes.append(codes)
+            q_scales.append(scales)
+            if n == 0:
+                key_scales = keep.tile([P, I], U8, name="key_scales", align_bytes=64)
+                nc.vector.tensor_copy(key_scales[:], key_scale_pool[:].indirect(offs_t[:]))
+            quantize(nc, codes[:], scales[:], grouped[:])
+        key_words = keep.tile([P, I], U32, name="key_words", align_bytes=64)
+        nc.vector.tensor_copy(key_words[:], key_word_pool[:].indirect(offs_t[:]))
+
+        factor_ps = psum.tile([P, PACK, P], F32, name="factor_ps", tag="turn")
+        for t in range(PACK):
+            nc.tensor.transpose(factor_ps[:, t, :], factor_col[:, t : t + 1].to_broadcast([P, P]), ident[:])
+        factor_row = keep.tile([P, P, PACK], F32, name="factor_row")
+        nc.scalar.copy(factor_row[:], factor_ps[:].rearrange("p t n -> p n t"))
+        mem_ps = psum.tile([P, 2, P], F32, name="mem_ps", tag="turn")
+        for t in range(2):
+            nc.tensor.transpose(mem_ps[:, t, :], mem_col[:, t : t + 1].to_broadcast([P, P]), ident[:])
+        mem_row = keep.tile([P, P, 2], F32, name="mem_row")
+        nc.scalar.copy(mem_row[:], mem_ps[:].rearrange("p t n -> p n t"))
+        mem_flat = mem_row[:].rearrange("p n t -> p (n t)")
+        carried = keep.tile([P, E_TILES, Q], F32, name="carried")
+        nc.vector.memset(carried[:, :, 0:1], 0.0)
+
+        b_sb, a_ps = [], []
+        for h in range(Q_TILES):
+            cols = slice(h * P, (h + 1) * P)
+            b_ps = psum.tile([P, I], F32, name="b_ps")
+            nc.tensor.matmul_mx(
+                out=b_ps[:], lhsT=q_codes[0][:, cols].bitcast(FP8X4), lhsT_scale=q_scales[0][:, cols],
+                rhs=note_codes[:].bitcast(FP8X4), rhs_scale=note_scales[:], start=True, stop=True,
+            )
+            b_copy = work.tile([P, I], F32, name="b_copy")
+            nc.scalar.copy(b_copy[:], b_ps[:])
+            b_sb.append(b_copy)
+        for h in range(Q_TILES):
+            cols = slice(h * P, (h + 1) * P)
+            a_bank = psum.tile([P, I], F32, name="a_bank")
+            nc.tensor.matmul_mx(
+                out=a_bank[:], lhsT=q_codes[1][:, cols].bitcast(FP8X4), lhsT_scale=q_scales[1][:, cols],
+                rhs=key_words[:].bitcast(FP8X4), rhs_scale=key_scales[:], start=True, stop=True,
+            )
+            a_ps.append(a_bank)
+
+        p_t, total = [], []
+        for h in range(Q_TILES):
+            larger = work.tile([P, I], F32, name="larger")
+            smaller = work.tile([P, I], F32, name="smaller")
+            nc.vector.tensor_tensor(larger[:], a_ps[h][:], b_sb[h][:], ALU.max)
+            nc.vector.tensor_tensor(smaller[:], a_ps[h][:], b_sb[h][:], ALU.min)
+            score = work.tile([P, I], F32, name="score")
+            nc.vector.scalar_tensor_tensor(score[:], smaller[:], lam_col[:, h : h + 1], larger[:], ALU.mult, ALU.add)
+            neg_max = work.tile([P, 1], F32, name="neg_max")
+            nc.vector.tensor_reduce(neg_max[:], score[:], AX.X, ALU.max, negate=True)
+            p = work.tile([P, I], F32, name="p")
+            p_sum = work.tile([P, 1], F32, name="p_sum")
+            nc.scalar.activation(p[:], score[:], ACT.Exp, bias=neg_max[:], scale=1.0, accum_out=p_sum[:])
+            p_t.append(p)
+            total.append(p_sum)
+
+        def turn_and_quantize(rows, codes, scales):
+            words = rows.bitcast(F32)
+            turned = psum.tile([P, 2, P], F32, name="turned", tag="turn")
+            for u in range(2):
+                nc.tensor.transpose(turned[:, u, :], words[:, u : I // 2 : 2], ident[:])
+            grouped = work.tile([P, P, PACK], BF16, name="turned_grouped", align_bytes=64)
+            nc.scalar.copy(
+                grouped[:].rearrange("p c t -> p (c t)").bitcast(F32).rearrange("p (c u) -> p c u", u=2),
+                turned[:].rearrange("p u c -> p c u"),
+            )
+            quantize(nc, codes, scales, grouped[:])
+
+        v_codes, v_scales = [], []
+
+        def prepare_values(j):
+            picked = work.tile([P, I], BF16, name="picked", align_bytes=64)
+            if j < E_TILES - 1:
+                nc.scalar.activation(picked[:], val_pool[j][:].indirect(offs_t[:]), ACT.Copy)
+            else:
+                nc.vector.tensor_copy(picked[:, :half], val_pool[j][:].indirect(offs_t[:, : half // 16]))
+                nc.scalar.activation(picked[:, half:], val_pool[j][:].indirect(offs_t[:, half // 16 :]), ACT.Copy)
+            codes = keep.tile([P, P], U32, name=f"v_codes{j}", align_bytes=64)
+            scales = keep.tile([P, P], U8, name=f"v_scales{j}", align_bytes=64)
+            turn_and_quantize(picked[:], codes[:], scales[:])
+            v_codes.append(codes)
+            v_scales.append(scales)
+
+        w_codes = keep.tile([P, Q], U32, name="w_codes", align_bytes=64)
+        w_scales = keep.tile([P, Q], U8, name="w_scales", align_bytes=64)
+        for h in range(Q_TILES):
+            p = p_t[h]
+            inv_sum = work.tile([P, 1], F32, name="inv_sum")
+            nc.vector.reciprocal(inv_sum[:], total[h][:])
+            run_sum = work.tile([P, G], F32, name="run_sum")
+            nc.vector.tensor_reduce(run_sum[:], p[:].rearrange("p (g r) -> p g r", r=RUN), AX.X, ALU.add)
+            damp_scale = work.tile([P, 1], F32, name="damp_scale")
+            nc.vector.tensor_scalar(damp_scale[:], inv_sum[:], shy_col[:, h : h + 1], -1.0, ALU.mult, ALU.mult)
+            damp = work.tile([P, G], F32, name="damp")
+            nc.scalar.activation(damp[:], run_sum[:], ACT.Exp, scale=damp_scale[:])
+            scaled = work.tile([P, I], F32, name="scaled")
+            nc.vector.tensor_tensor(scaled[:], p[:], factor_row[:].rearrange("p n t -> p (n t)"), ALU.mult)
+            damped_runs = work.tile([P, G], F32, name="damped_runs")
+            damped_sum = work.tile([P, 1], F32, name="damped_sum")
+            nc.vector.scalar_tensor_tensor(
+                damped_runs[:], damp[:], 1.0, run_sum[:], ALU.mult, ALU.mult, accum_out=damped_sum[:]
+            )
+            inv_damped = work.tile([P, 1], F32, name="inv_damped")
+            nc.vector.reciprocal(inv_damped[:], damped_sum[:])
+            weights = work.tile([P, I], BF16, name="weights", align_bytes=64)
+            nc.vector.scalar_tensor_tensor(
+                weights[:].rearrange("p (g r) -> p g r", r=RUN),
+                scaled[:].rearrange("p (g r) -> p g r", r=RUN),
+                inv_damped[:],
+                damp[:].unsqueeze(2).to_broadcast([P, G, RUN]),
+                ALU.mult,
+                ALU.mult,
+            )
+            cols = slice(h * P, (h + 1) * P)
+            turn_and_quantize(weights[:], w_codes[:, cols], w_scales[:, cols])
+            prepare_values(h)
+        for j in range(Q_TILES, E_TILES):
+            prepare_values(j)
+
+        for j in range(E_TILES):
+            o_ps = psum.tile([P, Q], F32, name="o_ps")
+            nc.tensor.matmul_mx(
+                out=o_ps[:], lhsT=v_codes[j][:].bitcast(FP8X4), lhsT_scale=v_scales[j][:],
+                rhs=w_codes[:].bitcast(FP8X4), rhs_scale=w_scales[:], start=True, stop=True,
+            )
+            nc.vector.tensor_tensor(carried[:, j, 1:], o_ps[:, : Q - 1], mem_flat[:, 1:], ALU.mult)
+            result = keep.tile([P, Q], F32, name=f"result{j}")
+            nc.vector.tensor_tensor(result[:], o_ps[:], carried[:, j, :], ALU.subtract)
+            nc.sync.dma_start(out=out[j * P : (j + 1) * P, :], in_=result[:])

@@ -49,20 +49,28 @@ def tile_attend_twopools_crowdshy_rowchanges_kernel(
         offs2_t = lists.tile([P, I // 16], U16, name="offs2_t")
 
         key_scale_pool = keep.tile([P, T], U8, name="key_scale_pool", align_bytes=64)
-        nc.vector.memset(key_scale_pool[:].bitcast(I32), 0)
+        nc.gpsimd.memset(key_scale_pool[:].bitcast(I32), 0)
+        rows = keep.tile([P, P], F32, name="rows")
+        nc.gpsimd.memset(rows[:], 0.0)
+        ident = keep.tile([P, P], F32, name="ident")
+        make_identity(nc, ident[:])
 
         notes_rows = notes.rearrange("(p t) u -> p t u", t=PACK)
         note_pool = [keep.tile([P, U], F32, name=f"note_pool{t}") for t in range(PACK)]
         nc.sync.dma_start(out=note_pool[0][:], in_=notes_rows[:, 0, :])
         nc.sync.dma_start(offs2_t[:], offs2)
-        for t in range(1, PACK):
-            nc.sync.dma_start(out=note_pool[t][:], in_=notes_rows[:, t, :])
         nc.sync.dma_start(offs_t[:], offs)
         for quad in range(4):
             nc.sync.dma_start(
                 out=key_scale_pool[32 * quad : 32 * quad + 4, :].bitcast(I32),
                 in_=keys_scales[0, 4 * quad : 4 * quad + 4, :].bitcast(I32),
             )
+        for t in range(1, PACK):
+            nc.sync.dma_start(out=note_pool[t][:], in_=notes_rows[:, t, :])
+        nc.sync.dma_start(out=rows[0:2, :], in_=lam.rearrange("(h p) o -> h (p o)", p=P))
+        nc.sync.dma_start(out=rows[2:4, :], in_=shy.rearrange("(h p) o -> h (p o)", p=P))
+        nc.sync.dma_start(out=rows[4:8, :], in_=slot_factor.rearrange("o (h p) -> (o h) p", p=P))
+        nc.sync.dma_start(out=rows[8:10, :], in_=memq.rearrange("o (h p) -> (o h) p", p=P))
         q2_raw = keep.tile([P, PACK, Q], F32, name="q2_raw")
         nc.sync.dma_start(out=q2_raw[:], in_=query2.rearrange("(p t) q -> p t q", t=PACK))
         q1_raw = keep.tile([P, PACK, Q], F32, name="q1_raw")
@@ -71,25 +79,15 @@ def tile_attend_twopools_crowdshy_rowchanges_kernel(
         nc.sync.dma_start(
             out=key_word_pool[:].bitcast(I32), in_=keys_words[0].rearrange("p n t -> p (n t)").bitcast(I32)
         )
-        lam_col = keep.tile([P, Q_TILES], F32, name="lam_col")
-        shy_col = keep.tile([P, Q_TILES], F32, name="shy_col")
-        with nc.allow_non_contiguous_dma(reason="one value a query row, rows on the partitions"):
-            nc.sync.dma_start(out=lam_col[:], in_=lam.rearrange("(h p) o -> p (h o)", p=P))
-            nc.sync.dma_start(out=shy_col[:], in_=shy.rearrange("(h p) o -> p (h o)", p=P))
-        factor_col = keep.tile([P, PACK], F32, name="factor_col")
-        nc.sync.dma_start(out=factor_col[:], in_=slot_factor.rearrange("o (p t) -> p (o t)", t=PACK))
-        mem_col = keep.tile([P, 2], F32, name="mem_col")
-        nc.sync.dma_start(out=mem_col[:], in_=memq.rearrange("o (p t) -> p (o t)", t=2))
-        val_pool = [keep.tile([P, T], F32, name=f"val_pool{j}") for j in range(E_TILES)]
+        val_pool = [keep.tile([P, T], F32, name=f"val_pool{j}", align_bytes=64) for j in range(E_TILES)]
         for j in range(E_TILES):
             nc.sync.dma_start(out=val_pool[j][:], in_=vals[j * P : (j + 1) * P, :])
-
-        ident = keep.tile([P, P], F32, name="ident")
-        make_identity(nc, ident[:])
 
         note_planes = keep.tile([P, PACK, I], BF16, name="note_planes", align_bytes=64)
         half = I // 2
         nc.vector.tensor_copy(note_planes[:, 0, :], note_pool[0][:].indirect(offs2_t[:]))
+        key_scales = keep.tile([P, I], U8, name="key_scales", align_bytes=64)
+        nc.vector.tensor_copy(key_scales[:], key_scale_pool[:].indirect(offs_t[:]))
         nc.scalar.activation(note_planes[:, 1, :], note_pool[1][:].indirect(offs2_t[:]), ACT.Copy)
         nc.vector.tensor_copy(note_planes[:, 2, :], note_pool[2][:].indirect(offs2_t[:]))
         nc.vector.tensor_copy(note_planes[:, 3, :half], note_pool[3][:].indirect(offs2_t[:, : half // 16]))
@@ -100,6 +98,18 @@ def tile_attend_twopools_crowdshy_rowchanges_kernel(
         note_scales = keep.tile([P, I], U8, name="note_scales", align_bytes=64)
         quantize(nc, note_codes[:], note_scales[:], note_grouped[:])
 
+        cols_ps = psum.tile([P, P], F32, name="cols_ps", tag="vec")
+        nc.tensor.transpose(cols_ps[:], rows[:], ident[:])
+        vec_cols = keep.tile([P, 10], F32, name="vec_cols")
+        nc.scalar.copy(vec_cols[:], cols_ps[:, :10])
+        lam_col, shy_col = vec_cols[:, 0:2], vec_cols[:, 2:4]
+        factor_ps = psum.tile([P, PACK, P], F32, name="factor_ps", tag="vec")
+        for t in range(PACK):
+            nc.tensor.transpose(factor_ps[:, t, :], vec_cols[:, 4 + t : 5 + t].to_broadcast([P, P]), ident[:])
+        mem_ps = psum.tile([P, 2, P], F32, name="mem_ps", tag="vec")
+        for t in range(2):
+            nc.tensor.transpose(mem_ps[:, t, :], vec_cols[:, 8 + t : 9 + t].to_broadcast([P, P]), ident[:])
+
         q_codes, q_scales = [], []
         for n, raw in enumerate((q2_raw, q1_raw)):
             grouped = keep.tile([P, Q, PACK], BF16, name=f"q_grouped{n}", align_bytes=64)
@@ -108,31 +118,20 @@ def tile_attend_twopools_crowdshy_rowchanges_kernel(
             scales = keep.tile([P, Q], U8, name=f"q_scales{n}", align_bytes=64)
             q_codes.append(codes)
             q_scales.append(scales)
-            if n == 0:
-                key_scales = keep.tile([P, I], U8, name="key_scales", align_bytes=64)
-                nc.vector.tensor_copy(key_scales[:], key_scale_pool[:].indirect(offs_t[:]))
             quantize(nc, codes[:], scales[:], grouped[:])
         key_words = keep.tile([P, I], U32, name="key_words", align_bytes=64)
         nc.vector.tensor_copy(key_words[:], key_word_pool[:].indirect(offs_t[:]))
-
-        factor_ps = psum.tile([P, PACK, P], F32, name="factor_ps", tag="turn")
-        for t in range(PACK):
-            nc.tensor.transpose(factor_ps[:, t, :], factor_col[:, t : t + 1].to_broadcast([P, P]), ident[:])
-        factor_row = keep.tile([P, P, PACK], F32, name="factor_row")
-        nc.scalar.copy(factor_row[:], factor_ps[:].rearrange("p t n -> p n t"))
-        mem_ps = psum.tile([P, 2, P], F32, name="mem_ps", tag="turn")
-        for t in range(2):
-            nc.tensor.transpose(mem_ps[:, t, :], mem_col[:, t : t + 1].to_broadcast([P, P]), ident[:])
-        mem_row = keep.tile([P, P, 2], F32, name="mem_row")
-        nc.scalar.copy(mem_row[:], mem_ps[:].rearrange("p t n -> p n t"))
-        mem_flat = mem_row[:].rearrange("p n t -> p (n t)")
+        spread = keep.tile([P, I + Q], F32, name="spread", tag="key_word_pool", align_bytes=64)
+        factor_row, mem_row = spread[:, :I], spread[:, I:]
+        nc.vector.tensor_copy(factor_row, factor_ps[:].rearrange("p t n -> p (t n)"))
+        nc.vector.tensor_copy(mem_row, mem_ps[:].rearrange("p t n -> p (t n)"))
         carried = keep.tile([P, E_TILES, Q], F32, name="carried")
         nc.vector.memset(carried[:, :, 0:1], 0.0)
 
         b_sb, a_ps = [], []
         for h in range(Q_TILES):
             cols = slice(h * P, (h + 1) * P)
-            b_ps = psum.tile([P, I], F32, name="b_ps")
+            b_ps = psum.tile([P, I], F32, name="b_ps", tag="b")
             nc.tensor.matmul_mx(
                 out=b_ps[:], lhsT=q_codes[0][:, cols].bitcast(FP8X4), lhsT_scale=q_scales[0][:, cols],
                 rhs=note_codes[:].bitcast(FP8X4), rhs_scale=note_scales[:], start=True, stop=True,
@@ -142,99 +141,125 @@ def tile_attend_twopools_crowdshy_rowchanges_kernel(
             b_sb.append(b_copy)
         for h in range(Q_TILES):
             cols = slice(h * P, (h + 1) * P)
-            a_bank = psum.tile([P, I], F32, name="a_bank")
+            a_bank = psum.tile([P, I], F32, name="a_bank", tag="a")
             nc.tensor.matmul_mx(
                 out=a_bank[:], lhsT=q_codes[1][:, cols].bitcast(FP8X4), lhsT_scale=q_scales[1][:, cols],
                 rhs=key_words[:].bitcast(FP8X4), rhs_scale=key_scales[:], start=True, stop=True,
             )
             a_ps.append(a_bank)
 
-        p_t, total = [], []
-        for h in range(Q_TILES):
-            larger = work.tile([P, I], F32, name="larger")
-            smaller = work.tile([P, I], F32, name="smaller")
-            nc.vector.tensor_tensor(larger[:], a_ps[h][:], b_sb[h][:], ALU.max)
-            nc.vector.tensor_tensor(smaller[:], a_ps[h][:], b_sb[h][:], ALU.min)
-            score = work.tile([P, I], F32, name="score")
-            nc.vector.scalar_tensor_tensor(score[:], smaller[:], lam_col[:, h : h + 1], larger[:], ALU.mult, ALU.add)
-            neg_max = work.tile([P, 1], F32, name="neg_max")
-            nc.vector.tensor_reduce(neg_max[:], score[:], AX.X, ALU.max, negate=True)
-            p = work.tile([P, I], F32, name="p")
-            p_sum = work.tile([P, 1], F32, name="p_sum")
-            nc.scalar.activation(p[:], score[:], ACT.Exp, bias=neg_max[:], scale=1.0, accum_out=p_sum[:])
-            p_t.append(p)
-            total.append(p_sum)
-
-        def turn_and_quantize(rows, codes, scales):
-            words = rows.bitcast(F32)
-            turned = psum.tile([P, 2, P], F32, name="turned", tag="turn")
-            for u in range(2):
-                nc.tensor.transpose(turned[:, u, :], words[:, u : I // 2 : 2], ident[:])
-            grouped = work.tile([P, P, PACK], BF16, name="turned_grouped", align_bytes=64)
+        def turn(sources, name, bank_tag, grouped_tag, codes_tag):
+            count = len(sources)
+            turned = psum.tile([P, count, 2, P], F32, name=f"turned_{name}", tag=bank_tag)
+            for n, source in enumerate(sources):
+                words = source.bitcast(F32)
+                for u in range(2):
+                    nc.tensor.transpose(turned[:, n, u, :], words[:, u : I // 2 : 2], ident[:])
+            grouped = keep.tile([P, count * P, PACK], BF16, name=f"grouped_{name}", tag=grouped_tag, align_bytes=64)
             nc.scalar.copy(
-                grouped[:].rearrange("p c t -> p (c t)").bitcast(F32).rearrange("p (c u) -> p c u", u=2),
-                turned[:].rearrange("p u c -> p c u"),
+                grouped[:].rearrange("p c t -> p (c t)").bitcast(F32).rearrange("p (n c u) -> p n c u", n=count, u=2),
+                turned[:].rearrange("p n u c -> p n c u"),
             )
-            quantize(nc, codes, scales, grouped[:])
+            codes = keep.tile([P, count * P], U32, name=f"codes_{name}", tag=codes_tag, align_bytes=64)
+            scales = keep.tile([P, count * P], U8, name=f"scales_{name}", align_bytes=64)
+            quantize(nc, codes[:], scales[:], grouped[:])
+            return [(codes[:, n * P : (n + 1) * P], scales[:, n * P : (n + 1) * P]) for n in range(count)]
 
-        v_codes, v_scales = [], []
+        def pick_values(j, tag):
+            picked = keep.tile([P, I], BF16, name=f"picked{j}", tag=tag, align_bytes=64)
+            nc.scalar.activation(picked[:], val_pool[j][:].indirect(offs_t[:]), ACT.Copy)
+            return picked[:]
 
-        def prepare_values(j):
-            picked = work.tile([P, I], BF16, name="picked", align_bytes=64)
-            if j < E_TILES - 1:
-                nc.scalar.activation(picked[:], val_pool[j][:].indirect(offs_t[:]), ACT.Copy)
-            else:
-                nc.vector.tensor_copy(picked[:, :half], val_pool[j][:].indirect(offs_t[:, : half // 16]))
-                nc.scalar.activation(picked[:, half:], val_pool[j][:].indirect(offs_t[:, half // 16 :]), ACT.Copy)
-            codes = keep.tile([P, P], U32, name=f"v_codes{j}", align_bytes=64)
-            scales = keep.tile([P, P], U8, name=f"v_scales{j}", align_bytes=64)
-            turn_and_quantize(picked[:], codes[:], scales[:])
-            v_codes.append(codes)
-            v_scales.append(scales)
+        def tiles_of(name, width, dtype=F32):
+            return [keep.tile([P, width], dtype, name=f"{name}{h}", align_bytes=64) for h in range(Q_TILES)]
 
-        w_codes = keep.tile([P, Q], U32, name="w_codes", align_bytes=64)
-        w_scales = keep.tile([P, Q], U8, name="w_scales", align_bytes=64)
+        larger, smaller, score, scaled = (tiles_of(n, I) for n in ("larger", "smaller", "score", "scaled"))
+        p = []
+        neg_max, p_sum, inv_sum, damp_scale, damped_sum, inv_damped = (
+            tiles_of(n, 1) for n in ("neg_max", "p_sum", "inv_sum", "damp_scale", "damped_sum", "inv_damped")
+        )
+        run_sum, damped_runs = tiles_of("run_sum", G), tiles_of("damped_runs", G)
+        weights = tiles_of("weights", I, BF16)
+
+        def pick_larger(h):
+            nc.vector.tensor_tensor(larger[h][:], a_ps[h][:], b_sb[h][:], ALU.max)
+
+        def pick_smaller(h):
+            nc.vector.tensor_tensor(smaller[h][:], a_ps[h][:], b_sb[h][:], ALU.min)
+
+        def join(h):
+            nc.vector.scalar_tensor_tensor(
+                score[h][:], smaller[h][:], lam_col[:, h : h + 1], larger[h][:], ALU.mult, ALU.add
+            )
+
+        def row_max_and_exp(h):
+            nc.vector.tensor_reduce(neg_max[h][:], score[h][:], AX.X, ALU.max, negate=True)
+            p.append(keep.tile([P, I], F32, name=f"p{h}", tag=("val_pool1", "p1")[h], align_bytes=64))
+            nc.scalar.activation(p[h][:], score[h][:], ACT.Exp, bias=neg_max[h][:], scale=1.0, accum_out=p_sum[h][:])
+
+        picked = [pick_values(0, "picked0")]
+        pick_larger(0)
+        pick_smaller(0)
+        pick_larger(1)
+        join(0)
+        pick_smaller(1)
+        picked.append(pick_values(1, "picked1"))
+        row_max_and_exp(0)
+        join(1)
+        v_mx = turn(picked[:1], "v0", "vturn", "grouped_v0", "smaller1")
+        row_max_and_exp(1)
+
+        damp = []
         for h in range(Q_TILES):
-            p = p_t[h]
-            inv_sum = work.tile([P, 1], F32, name="inv_sum")
-            nc.vector.reciprocal(inv_sum[:], total[h][:])
-            run_sum = work.tile([P, G], F32, name="run_sum")
-            nc.vector.tensor_reduce(run_sum[:], p[:].rearrange("p (g r) -> p g r", r=RUN), AX.X, ALU.add)
-            damp_scale = work.tile([P, 1], F32, name="damp_scale")
-            nc.vector.tensor_scalar(damp_scale[:], inv_sum[:], shy_col[:, h : h + 1], -1.0, ALU.mult, ALU.mult)
-            damp = work.tile([P, G], F32, name="damp")
-            nc.scalar.activation(damp[:], run_sum[:], ACT.Exp, scale=damp_scale[:])
-            scaled = work.tile([P, I], F32, name="scaled")
-            nc.vector.tensor_tensor(scaled[:], p[:], factor_row[:].rearrange("p n t -> p (n t)"), ALU.mult)
-            damped_runs = work.tile([P, G], F32, name="damped_runs")
-            damped_sum = work.tile([P, 1], F32, name="damped_sum")
+            nc.vector.reciprocal(inv_sum[h][:], p_sum[h][:])
+            nc.vector.tensor_reduce(run_sum[h][:], p[h][:].rearrange("p (g r) -> p g r", r=RUN), AX.X, ALU.add)
+            nc.vector.tensor_scalar(damp_scale[h][:], inv_sum[h][:], shy_col[:, h : h + 1], -1.0, ALU.mult, ALU.mult)
+            damp_h = keep.tile([P, G], F32, name=f"damp{h}", tag=("damp0", "val_pool2")[h], align_bytes=64)
+            nc.scalar.activation(damp_h[:], run_sum[h][:], ACT.Exp, scale=damp_scale[h][:])
+            damp.append(damp_h)
+            picked.append(pick_values(2 + h, f"damp_scale{h}"))
+        v_mx = v_mx + turn(picked[1:2], "v1", "vturn", "neg_max1", "inv_sum1")
+        for h in range(Q_TILES):
+            nc.vector.tensor_tensor(scaled[h][:], p[h][:], factor_row, ALU.mult)
+        for h in range(Q_TILES):
             nc.vector.scalar_tensor_tensor(
-                damped_runs[:], damp[:], 1.0, run_sum[:], ALU.mult, ALU.mult, accum_out=damped_sum[:]
+                damped_runs[h][:], damp[h][:], 1.0, run_sum[h][:], ALU.mult, ALU.mult, accum_out=damped_sum[h][:]
             )
-            inv_damped = work.tile([P, 1], F32, name="inv_damped")
-            nc.vector.reciprocal(inv_damped[:], damped_sum[:])
-            weights = work.tile([P, I], BF16, name="weights", align_bytes=64)
+        for h in range(Q_TILES):
+            nc.vector.reciprocal(inv_damped[h][:], damped_sum[h][:])
+        for h in range(Q_TILES):
             nc.vector.scalar_tensor_tensor(
-                weights[:].rearrange("p (g r) -> p g r", r=RUN),
-                scaled[:].rearrange("p (g r) -> p g r", r=RUN),
-                inv_damped[:],
-                damp[:].unsqueeze(2).to_broadcast([P, G, RUN]),
+                weights[h][:].rearrange("p (g r) -> p g r", r=RUN),
+                scaled[h][:].rearrange("p (g r) -> p g r", r=RUN),
+                inv_damped[h][:],
+                damp[h][:].unsqueeze(2).to_broadcast([P, G, RUN]),
                 ALU.mult,
                 ALU.mult,
             )
-            cols = slice(h * P, (h + 1) * P)
-            turn_and_quantize(weights[:], w_codes[:, cols], w_scales[:, cols])
-            prepare_values(h)
-        for j in range(Q_TILES, E_TILES):
-            prepare_values(j)
+        v_mx = v_mx + turn(picked[2:3], "v2", "vturn", "val_pool3", "inv_damped1")
+        v_mx = v_mx + turn(picked[3:], "v3", "vturn", "grouped_v3", "val_pool2")
+        w_mx = turn([weights[0][:]], "w0", "a", "damp_scale1", "scaled1")
+        w_mx = w_mx + turn([weights[1][:]], "w1", "a", "grouped_w1", "codes_w1")
 
-        for j in range(E_TILES):
-            o_ps = psum.tile([P, Q], F32, name="o_ps")
-            nc.tensor.matmul_mx(
-                out=o_ps[:], lhsT=v_codes[j][:].bitcast(FP8X4), lhsT_scale=v_scales[j][:],
-                rhs=w_codes[:].bitcast(FP8X4), rhs_scale=w_scales[:], start=True, stop=True,
-            )
-            nc.vector.tensor_tensor(carried[:, j, 1:], o_ps[:, : Q - 1], mem_flat[:, 1:], ALU.mult)
-            result = keep.tile([P, Q], F32, name=f"result{j}")
-            nc.vector.tensor_tensor(result[:], o_ps[:], carried[:, j, :], ALU.subtract)
-            nc.sync.dma_start(out=out[j * P : (j + 1) * P, :], in_=result[:])
+        out_tiles = out.rearrange("(j p) q -> p j q", p=P)
+        for h in range(Q_TILES):
+            for pair in range(E_TILES // 2):
+                tiles = slice(2 * pair, 2 * pair + 2)
+                o_ps = psum.tile([P, 2, P], F32, name="o_ps", tag=("b", "vec")[pair])
+                for n in range(2):
+                    v_codes, v_scales = v_mx[2 * pair + n]
+                    nc.tensor.matmul_mx(
+                        out=o_ps[:, n, :], lhsT=v_codes.bitcast(FP8X4), lhsT_scale=v_scales,
+                        rhs=w_mx[h][0].bitcast(FP8X4), rhs_scale=w_mx[h][1], start=True, stop=True,
+                    )
+                first = h * P + 1
+                count = min(P, Q - first)
+                nc.vector.tensor_tensor(
+                    carried[:, tiles, first : first + count],
+                    o_ps[:, :, :count],
+                    mem_row[:, first : first + count].unsqueeze(1).to_broadcast([P, 2, count]),
+                    ALU.mult,
+                )
+                result = keep.tile([P, 2, P], F32, name=f"result{h}{pair}")
+                nc.vector.tensor_tensor(result[:], o_ps[:], carried[:, tiles, h * P : (h + 1) * P], ALU.subtract)
+                nc.sync.dma_start(out=out_tiles[:, tiles, h * P : (h + 1) * P], in_=result[:])

@@ -43,7 +43,7 @@ def tile_attend_twopools_crowdshy_rowchanges_kernel(
         lists = ctx.enter_context(tc.tile_pool(name="lists", bufs=1))
         keep = ctx.enter_context(tc.tile_pool(name="keep", bufs=1))
         work = ctx.enter_context(tc.tile_pool(name="work", bufs=2))
-        psum = ctx.enter_context(tc.psum_pool(name="psum", bufs=2))
+        psum = ctx.enter_context(tc.psum_pool(name="psum", bufs=1))
 
         offs_t = lists.tile([P, I // 16], U16, name="offs_t")
         offs2_t = lists.tile([P, I // 16], U16, name="offs2_t")
@@ -93,34 +93,36 @@ def tile_attend_twopools_crowdshy_rowchanges_kernel(
         nc.vector.tensor_copy(note_planes[:, 3, :half], note_pool[3][:].indirect(offs2_t[:, : half // 16]))
         nc.scalar.activation(note_planes[:, 3, half:], note_pool[3][:].indirect(offs2_t[:, half // 16 :]), ACT.Copy)
         note_grouped = keep.tile([P, I, PACK], BF16, name="note_grouped", align_bytes=64)
-        interleave(nc.vector.tensor_copy, note_grouped[:], note_planes[:])
+        for part in (slice(0, half), slice(half, I)):
+            interleave(nc.vector.tensor_copy, note_grouped[:, part, :], note_planes[:, :, part])
         note_codes = keep.tile([P, I], U32, name="note_codes", align_bytes=64)
         note_scales = keep.tile([P, I], U8, name="note_scales", align_bytes=64)
         quantize(nc, note_codes[:], note_scales[:], note_grouped[:])
 
-        cols_ps = psum.tile([P, P], F32, name="cols_ps", tag="vec")
+        cols_ps = psum.tile([P, P], F32, name="cols_ps", tag="bank4")
         nc.tensor.transpose(cols_ps[:], rows[:], ident[:])
         vec_cols = keep.tile([P, 10], F32, name="vec_cols")
         nc.scalar.copy(vec_cols[:], cols_ps[:, :10])
         lam_col, shy_col = vec_cols[:, 0:2], vec_cols[:, 2:4]
-        factor_ps = psum.tile([P, PACK, P], F32, name="factor_ps", tag="vec")
+        factor_ps = psum.tile([P, PACK, P], F32, name="factor_ps", tag="bank5")
         for t in range(PACK):
             nc.tensor.transpose(factor_ps[:, t, :], vec_cols[:, 4 + t : 5 + t].to_broadcast([P, P]), ident[:])
-        mem_ps = psum.tile([P, 2, P], F32, name="mem_ps", tag="vec")
+        mem_ps = psum.tile([P, 2, P], F32, name="mem_ps", tag="bank4")
         for t in range(2):
             nc.tensor.transpose(mem_ps[:, t, :], vec_cols[:, 8 + t : 9 + t].to_broadcast([P, P]), ident[:])
 
         q_codes, q_scales = [], []
         for n, raw in enumerate((q2_raw, q1_raw)):
             grouped = keep.tile([P, Q, PACK], BF16, name=f"q_grouped{n}", align_bytes=64)
-            interleave(nc.scalar.copy, grouped[:], raw[:])
+            interleave((nc.vector.tensor_copy, nc.scalar.copy)[n], grouped[:], raw[:])
             codes = keep.tile([P, Q], U32, name=f"q_codes{n}", align_bytes=64)
             scales = keep.tile([P, Q], U8, name=f"q_scales{n}", align_bytes=64)
             q_codes.append(codes)
             q_scales.append(scales)
             quantize(nc, codes[:], scales[:], grouped[:])
         key_words = keep.tile([P, I], U32, name="key_words", align_bytes=64)
-        nc.vector.tensor_copy(key_words[:], key_word_pool[:].indirect(offs_t[:]))
+        nc.vector.tensor_copy(key_words[:, :half], key_word_pool[:].indirect(offs_t[:, : half // 16]))
+        nc.vector.tensor_copy(key_words[:, half:], key_word_pool[:].indirect(offs_t[:, half // 16 :]))
         spread = keep.tile([P, I + Q], F32, name="spread", tag="key_word_pool", align_bytes=64)
         factor_row, mem_row = spread[:, :I], spread[:, I:]
         nc.vector.tensor_copy(factor_row, factor_ps[:].rearrange("p t n -> p (t n)"))
@@ -131,7 +133,7 @@ def tile_attend_twopools_crowdshy_rowchanges_kernel(
         b_sb, a_ps = [], []
         for h in range(Q_TILES):
             cols = slice(h * P, (h + 1) * P)
-            b_ps = psum.tile([P, I], F32, name="b_ps", tag="b")
+            b_ps = psum.tile([P, I], F32, name="b_ps", tag=f"bank{h}")
             nc.tensor.matmul_mx(
                 out=b_ps[:], lhsT=q_codes[0][:, cols].bitcast(FP8X4), lhsT_scale=q_scales[0][:, cols],
                 rhs=note_codes[:].bitcast(FP8X4), rhs_scale=note_scales[:], start=True, stop=True,
@@ -141,11 +143,12 @@ def tile_attend_twopools_crowdshy_rowchanges_kernel(
             b_sb.append(b_copy)
         for h in range(Q_TILES):
             cols = slice(h * P, (h + 1) * P)
-            a_bank = psum.tile([P, I], F32, name="a_bank", tag="a")
-            nc.tensor.matmul_mx(
-                out=a_bank[:], lhsT=q_codes[1][:, cols].bitcast(FP8X4), lhsT_scale=q_scales[1][:, cols],
-                rhs=key_words[:].bitcast(FP8X4), rhs_scale=key_scales[:], start=True, stop=True,
-            )
+            a_bank = psum.tile([P, I], F32, name="a_bank", tag=f"bank{2 + h}")
+            for part in (slice(0, half), slice(half, I)):
+                nc.tensor.matmul_mx(
+                    out=a_bank[:, part], lhsT=q_codes[1][:, cols].bitcast(FP8X4), lhsT_scale=q_scales[1][:, cols],
+                    rhs=key_words[:, part].bitcast(FP8X4), rhs_scale=key_scales[:, part], start=True, stop=True,
+                )
             a_ps.append(a_bank)
 
         def turn(sources, name, bank_tag, grouped_tag, codes_tag):
@@ -206,7 +209,7 @@ def tile_attend_twopools_crowdshy_rowchanges_kernel(
         picked.append(pick_values(1, "picked1"))
         row_max_and_exp(0)
         join(1)
-        v_mx = turn(picked[:1], "v0", "vturn", "grouped_v0", "smaller1")
+        v_mx = turn(picked[:1], "v0", "bank6", "grouped_v0", "smaller1")
         row_max_and_exp(1)
 
         damp = []
@@ -218,16 +221,14 @@ def tile_attend_twopools_crowdshy_rowchanges_kernel(
             nc.scalar.activation(damp_h[:], run_sum[h][:], ACT.Exp, scale=damp_scale[h][:])
             damp.append(damp_h)
             picked.append(pick_values(2 + h, f"damp_scale{h}"))
-        v_mx = v_mx + turn(picked[1:2], "v1", "vturn", "neg_max1", "inv_sum1")
+        v_mx = v_mx + turn(picked[1:2], "v1", "bank7", "neg_max0", "inv_sum1")
         for h in range(Q_TILES):
-            nc.vector.tensor_tensor(scaled[h][:], p[h][:], factor_row, ALU.mult)
+            nc.gpsimd.tensor_tensor(scaled[h][:], p[h][:], factor_row, ALU.mult)
         for h in range(Q_TILES):
             nc.vector.scalar_tensor_tensor(
                 damped_runs[h][:], damp[h][:], 1.0, run_sum[h][:], ALU.mult, ALU.mult, accum_out=damped_sum[h][:]
             )
-        for h in range(Q_TILES):
             nc.vector.reciprocal(inv_damped[h][:], damped_sum[h][:])
-        for h in range(Q_TILES):
             nc.vector.scalar_tensor_tensor(
                 weights[h][:].rearrange("p (g r) -> p g r", r=RUN),
                 scaled[h][:].rearrange("p (g r) -> p g r", r=RUN),
@@ -236,30 +237,36 @@ def tile_attend_twopools_crowdshy_rowchanges_kernel(
                 ALU.mult,
                 ALU.mult,
             )
-        v_mx = v_mx + turn(picked[2:3], "v2", "vturn", "val_pool3", "inv_damped1")
-        v_mx = v_mx + turn(picked[3:], "v3", "vturn", "grouped_v3", "val_pool2")
-        w_mx = turn([weights[0][:]], "w0", "a", "damp_scale1", "scaled1")
-        w_mx = w_mx + turn([weights[1][:]], "w1", "a", "grouped_w1", "codes_w1")
+        w_mx = turn([weights[0][:]], "w0", "bank2", "val_pool3", "scaled1")
+        v_mx = v_mx + turn(picked[2:3], "v2", "bank6", "damp_scale1", "val_pool2")
+        v_mx = v_mx + turn(picked[3:], "v3", "bank7", "grouped_v3", "inv_damped1")
+        w_mx = w_mx + turn([weights[1][:]], "w1", "bank3", "grouped_w1", "codes_w1")
 
         out_tiles = out.rearrange("(j p) q -> p j q", p=P)
+        pairs = [slice(2 * pair, 2 * pair + 2) for pair in range(E_TILES // 2)]
         for h in range(Q_TILES):
-            for pair in range(E_TILES // 2):
-                tiles = slice(2 * pair, 2 * pair + 2)
-                o_ps = psum.tile([P, 2, P], F32, name="o_ps", tag=("b", "vec")[pair])
+            banks = []
+            for pair in range(len(pairs)):
+                o_ps = psum.tile([P, 2, P], F32, name="o_ps", tag=(("bank0", "bank3"), ("bank1", "bank4"))[h][pair])
                 for n in range(2):
                     v_codes, v_scales = v_mx[2 * pair + n]
                     nc.tensor.matmul_mx(
                         out=o_ps[:, n, :], lhsT=v_codes.bitcast(FP8X4), lhsT_scale=v_scales,
                         rhs=w_mx[h][0].bitcast(FP8X4), rhs_scale=w_mx[h][1], start=True, stop=True,
                     )
-                first = h * P + 1
-                count = min(P, Q - first)
+                banks.append(o_ps)
+            first = h * P + 1
+            count = min(P, Q - first)
+            for pair, tiles in enumerate(pairs):
                 nc.vector.tensor_tensor(
                     carried[:, tiles, first : first + count],
-                    o_ps[:, :, :count],
+                    banks[pair][:, :, :count],
                     mem_row[:, first : first + count].unsqueeze(1).to_broadcast([P, 2, count]),
                     ALU.mult,
                 )
+            for pair, tiles in enumerate(pairs):
                 result = keep.tile([P, 2, P], F32, name=f"result{h}{pair}")
-                nc.vector.tensor_tensor(result[:], o_ps[:], carried[:, tiles, h * P : (h + 1) * P], ALU.subtract)
+                nc.vector.tensor_tensor(
+                    result[:], banks[pair][:], carried[:, tiles, h * P : (h + 1) * P], ALU.subtract
+                )
                 nc.sync.dma_start(out=out_tiles[:, tiles, h * P : (h + 1) * P], in_=result[:])

from contextlib import ExitStack

import concourse.mybir as mybir
from concourse.masks import make_identity

D, T, I, Q, E, U, G = 512, 2048, 512, 256, 512, 1024, 64
FLOPS = 2 * (2 * D * Q * I + I * E * Q)

F32 = mybir.dt.float32
BF16 = mybir.dt.bfloat16
I32 = mybir.dt.int32
U32 = mybir.dt.uint32
U16 = mybir.dt.uint16
U8 = mybir.dt.uint8
FP8X4 = mybir.dt.float8_e4m3fn_x4
ALU = mybir.AluOpType
ACT = mybir.ActivationFunctionType
AX = mybir.AxisListType

P = 128
PACK = 4
RUN = I // G
Q_TILES = Q // P
E_TILES = E // P


def interleave(engine_copy, grouped, planes):
    engine_copy(
        out=grouped.rearrange("p (c i) t -> p c t i", i=4),
        in_=planes.rearrange("p t (c i) -> p c t i", i=4),
    )


def quantize(nc, codes, scales, grouped):
    nc.vector.quantize_mx(out=codes.bitcast(FP8X4), scales=scales, in_=grouped.rearrange("p c t -> p (c t)"))


def tile_attend_twopools_crowdshy_rowchanges_kernel(
    tc, query, keys_words, keys_scales, query2, notes, lam, shy, slot_factor, vals, memq, offs, offs2, out
):
    nc = tc.nc
    with ExitStack() as ctx:
        lists = ctx.enter_context(tc.tile_pool(name="lists", bufs=1))
        keep = ctx.enter_context(tc.tile_pool(name="keep", bufs=1))
        work = ctx.enter_context(tc.tile_pool(name="work", bufs=2))
        psum = ctx.enter_context(tc.psum_pool(name="psum", bufs=1))

        offs_t = lists.tile([P, I // 16], U16, name="offs_t")
        offs2_t = lists.tile([P, I // 16], U16, name="offs2_t")

        key_scale_pool = keep.tile([P, T], U8, name="key_scale_pool", align_bytes=64)
        nc.gpsimd.memset(key_scale_pool[:].bitcast(I32), 0)
        rows = keep.tile([P, P], F32, name="rows")
        nc.gpsimd.memset(rows[:], 0.0)
        ident = keep.tile([P, P], F32, name="ident")
        make_identity(nc, ident[:])

        notes_rows = notes.rearrange("(p t) u -> p t u", t=PACK)
        note_pool = [keep.tile([P, U], F32, name=f"note_pool{t}") for t in range(PACK)]
        nc.sync.dma_start(out=note_pool[0][:], in_=notes_rows[:, 0, :])
        nc.sync.dma_start(offs2_t[:], offs2)
        nc.sync.dma_start(offs_t[:], offs)
        for quad in range(4):
            nc.sync.dma_start(
                out=key_scale_pool[32 * quad : 32 * quad + 4, :].bitcast(I32),
                in_=keys_scales[0, 4 * quad : 4 * quad + 4, :].bitcast(I32),
            )
        for t in range(1, PACK):
            nc.sync.dma_start(out=note_pool[t][:], in_=notes_rows[:, t, :])
        nc.sync.dma_start(out=rows[0:2, :], in_=lam.rearrange("(h p) o -> h (p o)", p=P))
        nc.sync.dma_start(out=rows[2:4, :], in_=shy.rearrange("(h p) o -> h (p o)", p=P))
        nc.sync.dma_start(out=rows[4:8, :], in_=slot_factor.rearrange("o (h p) -> (o h) p", p=P))
        nc.sync.dma_start(out=rows[8:10, :], in_=memq.rearrange("o (h p) -> (o h) p", p=P))
        q2_raw = keep.tile([P, PACK, Q], F32, name="q2_raw")
        nc.sync.dma_start(out=q2_raw[:], in_=query2.rearrange("(p t) q -> p t q", t=PACK))
        q1_raw = keep.tile([P, PACK, Q], F32, name="q1_raw")
        nc.sync.dma_start(out=q1_raw[:], in_=query.rearrange("(p t) q -> p t q", t=PACK))
        key_word_pool = keep.tile([P, T], U32, name="key_word_pool", align_bytes=64)
        nc.sync.dma_start(
            out=key_word_pool[:].bitcast(I32), in_=keys_words[0].rearrange("p n t -> p (n t)").bitcast(I32)
        )
        val_pool = [keep.tile([P, T], F32, name=f"val_pool{j}", align_bytes=64) for j in range(E_TILES)]
        for j in range(E_TILES):
            nc.sync.dma_start(out=val_pool[j][:], in_=vals[j * P : (j + 1) * P, :])

        note_planes = keep.tile([P, PACK, I], BF16, name="note_planes", align_bytes=64)
        half = I // 2
        nc.vector.tensor_copy(note_planes[:, 0, :], note_pool[0][:].indirect(offs2_t[:]))
        key_scales = keep.tile([P, I], U8, name="key_scales", align_bytes=64)
        nc.vector.tensor_copy(key_scales[:], key_scale_pool[:].indirect(offs_t[:]))
        nc.scalar.activation(note_planes[:, 1, :], note_pool[1][:].indirect(offs2_t[:]), ACT.Copy)
        nc.vector.tensor_copy(note_planes[:, 2, :], note_pool[2][:].indirect(offs2_t[:]))
        nc.vector.tensor_copy(note_planes[:, 3, :half], note_pool[3][:].indirect(offs2_t[:, : half // 16]))
        nc.scalar.activation(note_planes[:, 3, half:], note_pool[3][:].indirect(offs2_t[:, half // 16 :]), ACT.Copy)
        note_grouped = keep.tile([P, I, PACK], BF16, name="note_grouped", align_bytes=64)
        for part in (slice(0, half), slice(half, I)):
            interleave(nc.vector.tensor_copy, note_grouped[:, part, :], note_planes[:, :, part])
        note_codes = keep.tile([P, I], U32, name="note_codes", align_bytes=64)
        note_scales = keep.tile([P, I], U8, name="note_scales", align_bytes=64)
        quantize(nc, note_codes[:], note_scales[:], note_grouped[:])

        cols_ps = psum.tile([P, P], F32, name="cols_ps", tag="bank4")
        nc.tensor.transpose(cols_ps[:], rows[:], ident[:])
        vec_cols = keep.tile([P, 10], F32, name="vec_cols")
        nc.scalar.copy(vec_cols[:], cols_ps[:, :10])
        lam_col, shy_col = vec_cols[:, 0:2], vec_cols[:, 2:4]
        factor_ps = psum.tile([P, PACK, P], F32, name="factor_ps", tag="bank5")
        for t in range(PACK):
            nc.tensor.transpose(factor_ps[:, t, :], vec_cols[:, 4 + t : 5 + t].to_broadcast([P, P]), ident[:])
        mem_ps = psum.tile([P, 2, P], F32, name="mem_ps", tag="bank4")
        for t in range(2):
            nc.tensor.transpose(mem_ps[:, t, :], vec_cols[:, 8 + t : 9 + t].to_broadcast([P, P]), ident[:])

        q_codes, q_scales = [], []
        for n, raw in enumerate((q2_raw, q1_raw)):
            grouped = keep.tile([P, Q, PACK], BF16, name=f"q_grouped{n}", align_bytes=64)
            interleave((nc.vector.tensor_copy, nc.scalar.copy)[n], grouped[:], raw[:])
            codes = keep.tile([P, Q], U32, name=f"q_codes{n}", align_bytes=64)
            scales = keep.tile([P, Q], U8, name=f"q_scales{n}", align_bytes=64)
            q_codes.append(codes)
            q_scales.append(scales)
            quantize(nc, codes[:], scales[:], grouped[:])
        key_words = keep.tile([P, I], U32, name="key_words", align_bytes=64)
        nc.vector.tensor_copy(key_words[:, :half], key_word_pool[:].indirect(offs_t[:, : half // 16]))
        nc.vector.tensor_copy(key_words[:, half:], key_word_pool[:].indirect(offs_t[:, half // 16 :]))
        spread = keep.tile([P, I + Q], F32, name="spread", tag="key_word_pool", align_bytes=64)
        factor_row, mem_row = spread[:, :I], spread[:, I:]
        nc.vector.tensor_copy(factor_row, factor_ps[:].rearrange("p t n -> p (t n)"))
        nc.vector.tensor_copy(mem_row, mem_ps[:].rearrange("p t n -> p (t n)"))
        carried = keep.tile([P, E_TILES, Q], F32, name="carried")
        nc.vector.memset(carried[:, :, 0:1], 0.0)

        b_sb, a_ps = [], []
        for h in range(Q_TILES):
            cols = slice(h * P, (h + 1) * P)
            b_ps = psum.tile([P, I], F32, name="b_ps", tag=f"bank{h}")
            nc.tensor.matmul_mx(
                out=b_ps[:], lhsT=q_codes[0][:, cols].bitcast(FP8X4), lhsT_scale=q_scales[0][:, cols],
                rhs=note_codes[:].bitcast(FP8X4), rhs_scale=note_scales[:], start=True, stop=True,
            )
            b_copy = work.tile([P, I], F32, name="b_copy")
            nc.scalar.copy(b_copy[:], b_ps[:])
            b_sb.append(b_copy)
        for h in range(Q_TILES):
            cols = slice(h * P, (h + 1) * P)
            a_bank = psum.tile([P, I], F32, name="a_bank", tag=f"bank{2 + h}")
            for part in (slice(0, half), slice(half, I)):
                nc.tensor.matmul_mx(
                    out=a_bank[:, part], lhsT=q_codes[1][:, cols].bitcast(FP8X4), lhsT_scale=q_scales[1][:, cols],
                    rhs=key_words[:, part].bitcast(FP8X4), rhs_scale=key_scales[:, part], start=True, stop=True,
                )
            a_ps.append(a_bank)

        def turn(sources, name, bank_tag, grouped_tag, codes_tag):
            count = len(sources)
            turned = psum.tile([P, count, 2, P], F32, name=f"turned_{name}", tag=bank_tag)
            for n, source in enumerate(sources):
                words = source.bitcast(F32)
                for u in range(2):
                    nc.tensor.transpose(turned[:, n, u, :], words[:, u : I // 2 : 2], ident[:])
            grouped = keep.tile([P, count * P, PACK], BF16, name=f"grouped_{name}", tag=grouped_tag, align_bytes=64)
            nc.scalar.copy(
                grouped[:].rearrange("p c t -> p (c t)").bitcast(F32).rearrange("p (n c u) -> p n c u", n=count, u=2),
                turned[:].rearrange("p n u c -> p n c u"),
            )
            codes = keep.tile([P, count * P], U32, name=f"codes_{name}", tag=codes_tag, align_bytes=64)
            scales = keep.tile([P, count * P], U8, name=f"scales_{name}", align_bytes=64)
            quantize(nc, codes[:], scales[:], grouped[:])
            return [(codes[:, n * P : (n + 1) * P], scales[:, n * P : (n + 1) * P]) for n in range(count)]

        def pick_values(j, tag):
            picked = keep.tile([P, I], BF16, name=f"picked{j}", tag=tag, align_bytes=64)
            nc.scalar.activation(picked[:], val_pool[j][:].indirect(offs_t[:]), ACT.Copy)
            return picked[:]

        def tiles_of(name, width, dtype=F32):
            return [keep.tile([P, width], dtype, name=f"{name}{h}", align_bytes=64) for h in range(Q_TILES)]

        larger, smaller, score, scaled = (tiles_of(n, I) for n in ("larger", "smaller", "score", "scaled"))
        p = []
        neg_max, p_sum, inv_sum, damp_scale, damped_sum, inv_damped = (
            tiles_of(n, 1) for n in ("neg_max", "p_sum", "inv_sum", "damp_scale", "damped_sum", "inv_damped")
        )
        run_sum, damped_runs = tiles_of("run_sum", G), tiles_of("damped_runs", G)
        weights = tiles_of("weights", I, BF16)

        def pick_larger(h):
            nc.vector.tensor_tensor(larger[h][:], a_ps[h][:], b_sb[h][:], ALU.max)

        def pick_smaller(h):
            nc.vector.tensor_tensor(smaller[h][:], a_ps[h][:], b_sb[h][:], ALU.min)

        def join(h):
            nc.vector.scalar_tensor_tensor(
                score[h][:], smaller[h][:], lam_col[:, h : h + 1], larger[h][:], ALU.mult, ALU.add
            )

        def row_max_and_exp(h):
            nc.vector.tensor_reduce(neg_max[h][:], score[h][:], AX.X, ALU.max, negate=True)
            p.append(keep.tile([P, I], F32, name=f"p{h}", tag=("val_pool1", "p1")[h], align_bytes=64))
            nc.scalar.activation(p[h][:], score[h][:], ACT.Exp, bias=neg_max[h][:], scale=1.0, accum_out=p_sum[h][:])

        picked = [pick_values(0, "picked0")]
        pick_larger(0)
        pick_smaller(0)
        pick_larger(1)
        join(0)
        pick_smaller(1)
        picked.append(pick_values(1, "picked1"))
        row_max_and_exp(0)
        join(1)
        v_mx = turn(picked[:1], "v0", "bank6", "grouped_v0", "smaller1")
        row_max_and_exp(1)

        damp = []
        for h in range(Q_TILES):
            nc.vector.reciprocal(inv_sum[h][:], p_sum[h][:])
            nc.vector.tensor_reduce(run_sum[h][:], p[h][:].rearrange("p (g r) -> p g r", r=RUN), AX.X, ALU.add)
            nc.vector.tensor_scalar(damp_scale[h][:], inv_sum[h][:], shy_col[:, h : h + 1], -1.0, ALU.mult, ALU.mult)
            damp_h = keep.tile([P, G], F32, name=f"damp{h}", tag=("damp0", "val_pool2")[h], align_bytes=64)
            nc.scalar.activation(damp_h[:], run_sum[h][:], ACT.Exp, scale=damp_scale[h][:])
            damp.append(damp_h)
            picked.append(pick_values(2 + h, f"damp_scale{h}"))
        v_mx = v_mx + turn(picked[1:2], "v1", "bank7", "neg_max0", "inv_sum1")
        for h in range(Q_TILES):
            nc.gpsimd.tensor_tensor(scaled[h][:], p[h][:], factor_row, ALU.mult)
        for h in range(Q_TILES):
            nc.vector.scalar_tensor_tensor(
                damped_runs[h][:], damp[h][:], 1.0, run_sum[h][:], ALU.mult, ALU.mult, accum_out=damped_sum[h][:]
            )
            nc.vector.reciprocal(inv_damped[h][:], damped_sum[h][:])
            nc.vector.scalar_tensor_tensor(
                weights[h][:].rearrange("p (g r) -> p g r", r=RUN),
                scaled[h][:].rearrange("p (g r) -> p g r", r=RUN),
                inv_damped[h][:],
                damp[h][:].unsqueeze(2).to_broadcast([P, G, RUN]),
                ALU.mult,
                ALU.mult,
            )
        w_mx = turn([weights[0][:]], "w0", "bank2", "val_pool3", "scaled1")
        v_mx = v_mx + turn(picked[2:3], "v2", "bank6", "damp_scale1", "val_pool2")
        v_mx = v_mx + turn(picked[3:], "v3", "bank7", "grouped_v3", "inv_damped1")
        w_mx = w_mx + turn([weights[1][:]], "w1", "bank3", "grouped_w1", "codes_w1")

        out_tiles = out.rearrange("(j p) q -> p j q", p=P)
        pairs = [slice(2 * pair, 2 * pair + 2) for pair in range(E_TILES // 2)]
        for h in range(Q_TILES):
            banks = []
            for pair in range(len(pairs)):
                o_ps = psum.tile([P, 2, P], F32, name="o_ps", tag=(("bank0", "bank3"), ("bank1", "bank4"))[h][pair])
                for n in range(2):
                    v_codes, v_scales = v_mx[2 * pair + n]
                    nc.tensor.matmul_mx(
                        out=o_ps[:, n, :], lhsT=v_codes.bitcast(FP8X4), lhsT_scale=v_scales,
                        rhs=w_mx[h][0].bitcast(FP8X4), rhs_scale=w_mx[h][1], start=True, stop=True,
                    )
                banks.append(o_ps)
            first = h * P + 1
            count = min(P, Q - first)
            for pair, tiles in enumerate(pairs):
                nc.vector.tensor_tensor(
                    carried[:, tiles, first : first + count],
                    banks[pair][:, :, :count],
                    mem_row[:, first : first + count].unsqueeze(1).to_broadcast([P, 2, count]),
                    ALU.mult,
                )
            for pair, tiles in enumerate(pairs):
                result = keep.tile([P, 2, P], F32, name=f"result{h}{pair}")
                nc.vector.tensor_tensor(
                    result[:], banks[pair][:], carried[:, tiles, h * P : (h + 1) * P], ALU.subtract
                )
                nc.sync.dma_start(out=out_tiles[:, tiles, h * P : (h + 1) * P], in_=result[:])
